import numpy as np
import ml_dtypes


def mxq(x, axis, fmt="e4m3"):
    dtype, down = {"e4m3": (ml_dtypes.float8_e4m3fn, 7), "e5m2": (ml_dtypes.float8_e5m2, 14)}[fmt]
    v = np.moveaxis(np.asarray(x, np.float32).astype(ml_dtypes.bfloat16).astype(np.float64), axis, -1)
    blocks = v.reshape(v.shape[:-1] + (-1, 32))
    amax = np.abs(blocks).max(-1, keepdims=True)
    byte = np.maximum(np.where(amax > 0, np.frexp(amax)[1] - 1 + 127, 0) - down, 1)
    scale = np.exp2(byte - 127.0)
    codes = (blocks / scale).astype(np.float32).astype(dtype).astype(np.float64)
    return np.moveaxis((codes * scale).reshape(v.shape), -1, axis)


WIDE = False


def mx_kscale(k):
    if not WIDE:
        return np.ones(k)
    levels = np.array([10, -10, 5, -5, 0])
    if k % 512:
        return np.exp2(np.random.permutation(np.resize(levels, k // 32))).repeat(32)
    a = np.empty((k // 512, 16))
    for p in range(k // 512):
        a[p, :8] = np.random.permutation(np.resize(levels, 8))
        for g in range(8):
            far = levels[np.abs(levels - a[p, g]) >= 10]
            a[p, g + 8] = far[np.random.randint(len(far))]
    return np.exp2(a.ravel()).repeat(32)


BF16 = ml_dtypes.bfloat16


def bf(x):
    return np.asarray(x, np.float32).astype(BF16)


def f64(x):
    return np.asarray(x).astype(np.float64)


G, M, F = 2, 1024, 512


def setup_inputs():
    s = mx_kscale(F)
    u = mx_kscale(M)
    x = np.random.standard_normal((G, M, F)) * s * u[:, None]
    c = 0.45 * np.random.standard_normal((G, F, F)) / np.sqrt(F) / s[:, None] * s
    m = 0.35 * np.random.standard_normal((G, M, M)) / np.sqrt(M) / u
    e = 0.35 * np.random.standard_normal((G, F, F)) / np.sqrt(F) / s[:, None]
    a = (1 + 0.1 * np.random.standard_normal((G, M))) / u
    v = (1 + 0.1 * np.random.standard_normal((G, F))) / s
    return {"x": bf(x), "c": bf(c), "m": bf(m), "e": bf(e), "a": bf(a), "v": bf(v)}


def reference(x, c, m, e, a, v):
    x = f64(x)
    z = mxq(x, 2, "e4m3") @ mxq(f64(c), 1, "e4m3")
    h = x + np.maximum(z, 0.0)
    r = mxq(f64(m), 2, "e4m3") @ mxq(h, 1, "e4m3")
    g = f64(a)[:, :, None] * h + r
    o = mxq(g, 2, "e4m3")[::-1] @ mxq(f64(e), 1, "e4m3")
    return f64(v)[:, None, :] * g + o

@@ -1,0 +1,499 @@
+from contextlib import ExitStack
+
+import concourse.mybir as mybir
+from concourse.masks import make_identity
+
+LEGS, FRAMES, CH = 2, 1024, 512
+FLOPS = 2 * LEGS * FRAMES * CH * (CH + FRAMES + CH)
+
+F32 = mybir.dt.float32
+BF16 = mybir.dt.bfloat16
+U32 = mybir.dt.uint32
+U8 = mybir.dt.uint8
+FP8X4 = mybir.dt.float8_e4m3fn_x4
+ADD = mybir.AluOpType.add
+MULT = mybir.AluOpType.mult
+MAX = mybir.AluOpType.max
+
+P = 128
+
+
+def tile_gait_leg_exchange_t1_kernel(tc, x, c, m, e, a, v, out):
+    nc = tc.nc
+    x_v = x.rearrange("l (g p t) c -> l g p t c", p=P, t=4)
+    m_v = m.rearrange("l (g p t) i -> l g p t i", p=P, t=4)
+    c_v = c.rearrange("l (p j) o -> l p j o", j=4)
+    e_v = e.rearrange("l (p j) o -> l p j o", j=4)
+    a_v = a.rearrange("l (g p t) -> p l g t", p=P, t=4)
+    out_v = out.rearrange("l (g p t) c -> l g t p c", p=P, t=4)
+
+    with ExitStack() as ctx:
+        keep = ctx.enter_context(tc.tile_pool(name="keep", bufs=1))
+        ring = ctx.enter_context(tc.tile_pool(name="ring", bufs=4))
+        tp_pool = ctx.enter_context(tc.psum_pool(name="tp_pool", bufs=4))
+        mm_pool = ctx.enter_context(tc.psum_pool(name="mm_pool", bufs=4))
+
+        def codes(name, width):
+            words = keep.tile([P, width], U32, name=name + "_codes", align_bytes=64)
+            scales = keep.tile([P, width], U8, name=name + "_scales", align_bytes=64)
+            return words, scales
+
+        ident = keep.tile([P, P], F32, name="ident", align_bytes=64)
+        a_b = keep.tile([P, LEGS, 2, 4], BF16, name="a_b", align_bytes=64)
+        a_f = keep.tile([P, LEGS * 8], F32, name="a_f", align_bytes=64)
+        v_t = keep.tile([P, LEGS, CH], BF16, name="v_t", align_bytes=64)
+        x_t, m_t, w_t, h_t = {}, {}, {}, {}
+        xq, mq, wq, hq, gq = {}, {}, {}, {}, {}
+        turned, tp, wT, hT, gT, vg_t = {}, {}, {}, {}, {}, {}
+        z_ps, r_ps, o_ps = {}, {}, {}
+
+        def load_x(l, g, parts=1):
+            x_t[l, g] = keep.tile([P, 4, CH], BF16, name="x%d%d" % (l, g), align_bytes=64)
+            n = 4 // parts
+            for i in range(parts):
+                nc.sync.dma_start(out=x_t[l, g][:, n * i : n * i + n, :], in_=x_v[l, g][:, n * i : n * i + n, :])
+
+        def load_m(l, g):
+            m_t[l, g] = ring.tile([P, 4, FRAMES], BF16, name="m_raw", tag="m_raw", bufs=4, align_bytes=64)
+            nc.sync.dma_start(out=m_t[l, g][:], in_=m_v[l, g])
+
+        def load_w(key, src):
+            w_t[key] = ring.tile([P, 4, CH], BF16, name="w_raw", tag="w_raw", bufs=3, align_bytes=64)
+            nc.sync.dma_start(out=w_t[key][:], in_=src)
+
+        def mx(dst, left, lcols, right, start, stop):
+            nc.tensor.matmul_mx(
+                out=dst,
+                lhsT=left[0][:, lcols].bitcast(FP8X4),
+                lhsT_scale=left[1][:, lcols],
+                rhs=right[0][:].bitcast(FP8X4),
+                rhs_scale=right[1][:],
+                start=start,
+                stop=stop,
+            )
+
+        def quant(dst, src):
+            nc.vector.quantize_mx(out=dst[0][:].bitcast(FP8X4), scales=dst[1][:], in_=src)
+
+        def bank(kind):
+            if kind == "tp":
+                return tp_pool.tile([P, CH], F32, name="tp", tag="tp")
+            return mm_pool.tile([P, CH], F32, name="mm", tag="mm")
+
+        def copy(eng, dst, src):
+            if eng == "S":
+                nc.scalar.copy(out=dst, in_=src)
+            elif eng == "V":
+                nc.vector.tensor_copy(out=dst, in_=src)
+            else:
+                nc.gpsimd.tensor_scalar(out=dst, in0=src, scalar1=1.0, scalar2=0.0, op0=MULT, op1=ADD)
+
+        def turn(key, src, base, half):
+            words = src[:].rearrange("p t k -> p (t k)").bitcast(F32).rearrange("p (t k) -> p t k", t=4)
+            if half == 0:
+                turned[key] = ring.tile([P, 4, P, 2], F32, name="turned", tag="turned", bufs=4, align_bytes=64)
+            tp[key, half] = bank("tp")
+            ps4 = tp[key, half][:].rearrange("p (t u f) -> p t u f", t=2, u=2)
+            for i in range(2):
+                for u in range(2):
+                    nc.tensor.transpose(ps4[:, i, u, :], words[:, 2 * half + i, base + u : base + 256 : 2], ident[:])
+
+        def turnc(key, half, eng):
+            ps4 = tp[key, half][:].rearrange("p (t u f) -> p t u f", t=2, u=2)
+            copy(eng, turned[key][:, 2 * half : 2 * half + 2, :, :], ps4.rearrange("p t u f -> p t f u"))
+
+        def tx(l, g, half):
+            turn(("x", l, g), x_t[l, g], 0, half)
+
+        def cx(l, g, half, eng="S"):
+            turnc(("x", l, g), half, eng)
+
+        def tm(l, g, k, half):
+            turn(("m", l, g, k), m_t[l, g], 256 * k, half)
+
+        def cm(l, g, k, half, eng="S"):
+            turnc(("m", l, g, k), half, eng)
+
+        def qx(l, g):
+            xq[l, g] = codes("x%d%d" % (l, g), CH)
+            quant(xq[l, g], turned["x", l, g][:].rearrange("p t f u -> p (t f u)").bitcast(BF16))
+
+        def qm(l, g, k):
+            mq[l, g, k] = codes("m%d%d%d" % (l, g, k), CH)
+            quant(mq[l, g, k], turned["m", l, g, k][:].rearrange("p t f u -> p (t f u)").bitcast(BF16))
+
+        def il_c(l, i, eng):
+            if i == 0:
+                wT["c", l] = ring.tile([P, CH, 4], BF16, name="w_grp", tag="w_grp", bufs=2, align_bytes=64)
+            dst = wT["c", l][:].rearrange("p (t q) j -> p t q j", t=4)
+            src = w_t["c", l][:].rearrange("p j (q t) -> p t q j", t=4)
+            copy(eng, dst[:, 2 * i : 2 * i + 2], src[:, 2 * i : 2 * i + 2])
+
+        def il_e(l, i, eng):
+            if i == 0:
+                wT["e", l] = ring.tile([P, CH, 4], BF16, name="w_grp", tag="w_grp", bufs=2, align_bytes=64)
+            dst = wT["e", l][:, 256 * i : 256 * i + 256, :].rearrange("p (q i) j -> p q j i", i=4)
+            src = w_t["e", l][:, :, 256 * i : 256 * i + 256].rearrange("p j (q i) -> p q j i", i=4)
+            copy(eng, dst, src)
+
+        def qw(key, l):
+            wq[key, l] = codes("%s%d" % (key, l), CH)
+            quant(wq[key, l], wT[key, l][:].rearrange("p o j -> p (o j)"))
+
+        def z(l, g, *ts):
+            for t in ts:
+                z_ps[l, g, t] = bank("mm")
+                mx(z_ps[l, g, t][:], xq[l, g], slice(P * t, P * t + P), wq["c", l], True, True)
+
+        def h(l, g, *ts):
+            for t in ts:
+                if t == 0:
+                    h_t[l, g] = keep.tile([P, 4, CH], F32, name="h%d%d" % (l, g), align_bytes=64)
+                nc.vector.scalar_tensor_tensor(
+                    out=h_t[l, g][:, t, :].rearrange("p (j q) -> p j q", j=4),
+                    in0=z_ps[l, g, t][:].rearrange("p (j q) -> p j q", j=4),
+                    scalar=0.0,
+                    in1=x_t[l, g][:, t, :].rearrange("p (q j) -> p j q", j=4),
+                    op0=MAX,
+                    op1=ADD,
+                )
+
+        def hb(l, g, i, eng):
+            if i == 0:
+                hT[l, g] = ring.tile([P, CH, 4], BF16, name="h_grp", tag="h_grp", bufs=3, align_bytes=64)
+            n = CH // 2
+            dst = hT[l, g][:, n * i : n * i + n, :].rearrange("p (q i) t -> p q t i", i=4)
+            src = h_t[l, g][:, :, n * i : n * i + n].rearrange("p t (q i) -> p q t i", i=4)
+            copy(eng, dst, src)
+
+        def qh(l, g):
+            hq[l, g] = codes("h%d%d" % (l, g), CH)
+            quant(hq[l, g], hT[l, g][:].rearrange("p o t -> p (o t)"))
+
+        def r(l, *ks):
+            for k in ks:
+                g_, t = divmod(k, 4)
+                r_ps[l, k] = bank("mm")
+                for kk in range(2):
+                    mx(r_ps[l, k][:], mq[l, g_, kk], slice(P * t, P * t + P), hq[l, kk], kk == 0, kk == 1)
+
+        def g(l, *ks):
+            for k in ks:
+                g_, t = divmod(k, 4)
+                nc.vector.scalar_tensor_tensor(
+                    out=h_t[l, g_][:, t, :],
+                    in0=h_t[l, g_][:, t, :],
+                    scalar=a_f[:, 8 * l + k : 8 * l + k + 1],
+                    in1=r_ps[l, k][:],
+                    op0=MULT,
+                    op1=ADD,
+                )
+
+        def vg(l, k, i, eng="G"):
+            g_, t = divmod(k, 4)
+            if i == 0:
+                vg_t[l, k] = ring.tile([P, CH], F32, name="vg", tag="vg", bufs=16, align_bytes=64)
+            q = slice(64 * i, 64 * i + 64)
+            (nc.vector if eng == "V" else nc.gpsimd).tensor_tensor(
+                out=vg_t[l, k][:].rearrange("p (q j) -> p q j", j=4)[:, q, :],
+                in0=h_t[l, g_][:, t, :].rearrange("p (j q) -> p q j", j=4)[:, q, :],
+                in1=v_t[:, l, :].rearrange("p (q j) -> p q j", j=4)[:, q, :],
+                op=MULT,
+            )
+
+        def tg(l, k):
+            g_, t = divmod(k, 4)
+            if k % 2 == 0:
+                gT[l, k // 2] = ring.tile([P, 2, P, 4], BF16, name="g_turned", tag="g_turned", bufs=4, align_bytes=64)
+            tp["g", l, k] = bank("tp")
+            for j in range(4):
+                nc.tensor.transpose(tp["g", l, k][:, P * j : P * j + P], h_t[l, g_][:, t, P * j : P * j + P], ident[:])
+
+        def cg(l, k):
+            nc.scalar.copy(out=gT[l, k // 2][:, k % 2], in_=tp["g", l, k][:].rearrange("p (j f) -> p f j", j=4))
+
+        def qg(l, k):
+            gq[l, k // 2] = codes("g%d%d" % (l, k // 2), 2 * P)
+            quant(gq[l, k // 2], gT[l, k // 2][:].rearrange("p i f j -> p (i f j)"))
+
+        def o(l, *ks):
+            for k in ks:
+                o_ps[l, k] = bank("mm")
+                mx(o_ps[l, k][:], gq[1 - l, k // 2], slice(P * (k % 2), P * (k % 2) + P), wq["e", l], True, True)
+
+        def y(l, *ks):
+            for k in ks:
+                g_, t = divmod(k, 4)
+                nc.vector.tensor_tensor(out=vg_t[l, k][:], in0=o_ps[l, k][:], in1=vg_t[l, k][:], op=ADD)
+                nc.sync.dma_start(out=out_v[l, g_, t], in_=vg_t[l, k][:])
+
+        with tc.manual_schedule():
+            nc.gpsimd.dma_start(out=a_b[:], in_=a_v)
+            make_identity(nc, ident[:])
+            nc.gpsimd.dma_start(out=v_t[:], in_=v.rearrange("l c -> (l c)").partition_broadcast(P))
+            nc.gpsimd.tensor_copy(out=a_f[:], in_=a_b[:].rearrange("p l g t -> p (l g t)"))
+            load_x(0, 0, 2)
+            load_w(("c", 0), c_v[0])
+            load_x(0, 1)
+            load_w(("c", 1), c_v[1])
+            load_x(1, 0)
+            load_x(1, 1)
+            load_m(0, 0)
+            load_m(0, 1)
+            load_w(("e", 0), e_v[0])
+            load_m(1, 0)
+            load_m(1, 1)
+
+            tx(0, 0, 0)
+            tx(0, 0, 1)
+            cx(0, 0, 0, "S")
+            cx(0, 0, 1, "V")
+            il_c(0, 0, "V")
+            il_c(0, 1, "V")
+            tx(0, 1, 0)
+            qx(0, 0)
+            tx(0, 1, 1)
+            cx(0, 1, 0, "S")
+            qw("c", 0)
+            cx(0, 1, 1, "S")
+            z(0, 0, 0)
+            il_c(1, 0, "S")
+            qx(0, 1)
+            z(0, 0, 1)
+            tx(1, 0, 0)
+            h(0, 0, 0)
+            tx(1, 0, 1)
+            h(0, 0, 1)
+            il_c(1, 1, "S")
+            z(0, 0, 2)
+            z(0, 0, 3)
+            h(0, 0, 2)
+            z(0, 1, 0)
+            cx(1, 0, 0, "S")
+            z(0, 1, 1)
+            h(0, 0, 3)
+            z(0, 1, 2)
+            cx(1, 0, 1, "S")
+            tx(1, 1, 0)
+            h(0, 1, 0)
+            z(0, 1, 3)
+            hb(0, 0, 0, "S")
+            h(0, 1, 1)
+            tx(1, 1, 1)
+            qw("c", 1)
+            hb(0, 0, 1, "S")
+            tm(0, 0, 0, 0)
+            qx(1, 0)
+            tm(0, 0, 0, 1)
+            h(0, 1, 2)
+            z(1, 0, 0)
+            cx(1, 1, 0, "S")
+            z(1, 0, 1)
+            h(0, 1, 3)
+            z(1, 0, 2)
+            cx(1, 1, 1, "S")
+            qh(0, 0)
+            hb(0, 1, 0, "G")
+            z(1, 0, 3)
+            cm(0, 0, 0, 0)
+            tm(0, 0, 1, 0)
+            h(1, 0, 0)
+            cm(0, 0, 0, 1)
+            h(1, 0, 1)
+            tm(0, 0, 1, 1)
+            hb(0, 1, 1, "G")
+            cm(0, 0, 1, 0)
+            tm(0, 1, 0, 0)
+            qx(1, 1)
+            cm(0, 0, 1, 1)
+            tm(0, 1, 0, 1)
+            h(1, 0, 2)
+            z(1, 1, 0)
+            cm(0, 1, 0, 0)
+            h(1, 0, 3)
+            z(1, 1, 1)
+            z(1, 1, 2)
+            il_e(0, 0, "S")
+            load_w(("e", 1), e_v[1])
+            h(1, 1, 0)
+            z(1, 1, 3)
+            h(1, 1, 1)
+            tm(0, 1, 1, 0)
+            hb(1, 0, 0, "S")
+            qm(0, 0, 0)
+            tm(0, 1, 1, 1)
+            h(1, 1, 2)
+            hb(1, 0, 1, "S")
+            h(1, 1, 3)
+            qh(0, 1)
+            hb(1, 1, 0, "G")
+            tm(1, 0, 0, 0)
+            qm(0, 0, 1)
+            cm(0, 1, 0, 1)
+            cm(0, 1, 1, 0)
+            qh(1, 0)
+            tm(1, 0, 0, 1)
+            r(0, 0)
+            hb(1, 1, 1, "G")
+            cm(0, 1, 1, 1)
+            r(0, 1)
+            qm(0, 1, 0)
+            r(0, 2)
+            cm(1, 0, 0, 0)
+            r(0, 3)
+            g(0, 0)
+            il_e(0, 1, "S")
+            g(0, 1)
+            vg(0, 0, 0)
+            tg(0, 0)
+            g(0, 2)
+            vg(0, 0, 1)
+            tg(0, 1)
+            g(0, 3)
+            cg(0, 0)
+            vg(0, 1, 0)
+            qm(0, 1, 1)
+            tg(0, 2)
+            cg(0, 1)
+            vg(0, 1, 1)
+            tg(0, 3)
+            cm(1, 0, 0, 1)
+            qh(1, 1)
+            r(0, 4)
+            vg(0, 2, 0)
+            r(0, 5)
+            cg(0, 2)
+            qg(0, 0)
+            vg(0, 2, 1)
+            g(0, 4)
+            cg(0, 3)
+            vg(0, 3, 0)
+            g(0, 5)
+            r(0, 6)
+            il_e(1, 0, "S")
+            r(0, 7)
+            qg(0, 2)
+            vg(0, 3, 1)
+            tg(0, 4)
+            g(0, 6)
+            tg(0, 5)
+            vg(0, 4, 0)
+            tm(1, 0, 1, 0)
+            cg(0, 4)
+            g(0, 7)
+            vg(0, 4, 1)
+            tm(1, 0, 1, 1)
+            cg(0, 5)
+            qm(1, 0, 0)
+            vg(0, 5, 0)
+            tg(0, 6)
+            cm(1, 0, 1, 0)
+            qw("e", 0)
+            tg(0, 7)
+            vg(0, 5, 1)
+            cm(1, 0, 1, 1)
+            qg(0, 4)
+            tm(1, 1, 0, 0)
+            vg(0, 6, 0)
+            cg(0, 6)
+            qm(1, 0, 1)
+            tm(1, 1, 0, 1)
+            cg(0, 7)
+            vg(0, 6, 1)
+            r(1, 0)
+            cm(1, 1, 0, 0)
+            vg(0, 7, 0)
+            qg(0, 6)
+            g(1, 0)
+            tm(1, 1, 1, 0)
+            cm(1, 1, 0, 1)
+            vg(0, 7, 1)
+            r(1, 1)
+            il_e(1, 1, "S")
+            tg(1, 0)
+            qm(1, 1, 0)
+            vg(1, 0, 0)
+            g(1, 1)
+            vg(1, 0, 1)
+            tm(1, 1, 1, 1)
+            cg(1, 0)
+            qw("e", 1)
+            vg(1, 1, 0)
+            tg(1, 1)
+            cm(1, 1, 1, 0)
+            vg(1, 1, 1)
+            cg(1, 1)
+            r(1, 2)
+            r(1, 3)
+            g(1, 2)
+            cm(1, 1, 1, 1)
+            o(1, 0)
+            o(1, 1)
+            g(1, 3)
+            vg(1, 2, 0)
+            tg(1, 2)
+            qm(1, 1, 1)
+            vg(1, 2, 1)
+            cg(1, 2)
+            tg(1, 3)
+            qg(1, 0)
+            vg(1, 3, 0)
+            r(1, 4)
+            y(1, 0)
+            cg(1, 3)
+            vg(1, 3, 1)
+            y(1, 1)
+            r(1, 5)
+            o(0, 0)
+            g(1, 4)
+            o(0, 1)
+            g(1, 5)
+            tg(1, 4)
+            vg(1, 4, 0)
+            o(1, 2)
+            qg(1, 2)
+            cg(1, 4)
+            vg(1, 4, 1)
+            y(0, 0)
+            tg(1, 5)
+            vg(1, 5, 0)
+            o(1, 3)
+            y(0, 1)
+            cg(1, 5)
+            vg(1, 5, 1)
+            y(1, 2)
+            r(1, 6)
+            y(1, 3)
+            o(0, 2)
+            r(1, 7)
+            g(1, 6)
+            o(0, 3)
+            g(1, 7)
+            tg(1, 6)
+            vg(1, 6, 0)
+            o(1, 4)
+            qg(1, 4)
+            cg(1, 6)
+            vg(1, 6, 1)
+            y(0, 2)
+            tg(1, 7)
+            vg(1, 7, 0)
+            o(1, 5)
+            y(0, 3)
+            cg(1, 7)
+            o(0, 4)
+            vg(1, 7, 1)
+            y(1, 4)
+            o(0, 5)
+            y(1, 5)
+            o(1, 6)
+            qg(1, 6)
+            o(1, 7)
+            y(0, 4)
+            y(0, 5)
+            o(0, 6)
+            y(1, 6)
+            o(0, 7)
+            y(1, 7)
+            y(0, 6)
+            y(0, 7)

@@ -14,6 +14,7 @@ FP8X4 = mybir.dt.float8_e4m3fn_x4
 ADD = mybir.AluOpType.add
 MULT = mybir.AluOpType.mult
 MAX = mybir.AluOpType.max
+COPY = mybir.ActivationFunctionType.Copy
 
 P = 128
 
@@ -25,6 +26,7 @@ def tile_gait_leg_exchange_t1_kernel(tc, x, c, m, e, a, v, out):
     c_v = c.rearrange("l (p j) o -> l p j o", j=4)
     e_v = e.rearrange("l (p j) o -> l p j o", j=4)
     a_v = a.rearrange("l (g p t) -> p l g t", p=P, t=4)
+    v_v = v.rearrange("l (p j) -> p l j", j=4)
     out_v = out.rearrange("l (g p t) c -> l g t p c", p=P, t=4)
 
     with ExitStack() as ctx:
@@ -42,9 +44,11 @@ def tile_gait_leg_exchange_t1_kernel(tc, x, c, m, e, a, v, out):
         a_b = keep.tile([P, LEGS, 2, 4], BF16, name="a_b", align_bytes=64)
         a_f = keep.tile([P, LEGS * 8], F32, name="a_f", align_bytes=64)
         v_t = keep.tile([P, LEGS, CH], BF16, name="v_t", align_bytes=64)
+        v_b = keep.tile([P, LEGS, 4], BF16, name="v_b", align_bytes=64)
+        v_f = keep.tile([P, LEGS * 4], F32, name="v_f", align_bytes=64)
         x_t, m_t, w_t, h_t = {}, {}, {}, {}
         xq, mq, wq, hq, gq = {}, {}, {}, {}, {}
-        turned, tp, wT, hT, gT, vg_t = {}, {}, {}, {}, {}, {}
+        turned, tp, wT, hT, gT, vg_t, oT = {}, {}, {}, {}, {}, {}, {}
         z_ps, r_ps, o_ps = {}, {}, {}
 
         def load_x(l, g, parts=1):
@@ -90,7 +94,7 @@ def tile_gait_leg_exchange_t1_kernel(tc, x, c, m, e, a, v, out):
 
         def turn(key, src, base, half):
             words = src[:].rearrange("p t k -> p (t k)").bitcast(F32).rearrange("p (t k) -> p t k", t=4)
-            if half == 0:
+            if key not in turned:
                 turned[key] = ring.tile([P, 4, P, 2], F32, name="turned", tag="turned", bufs=4, align_bytes=64)
             tp[key, half] = bank("tp")
             ps4 = tp[key, half][:].rearrange("p (t u f) -> p t u f", t=2, u=2)
@@ -123,18 +127,18 @@ def tile_gait_leg_exchange_t1_kernel(tc, x, c, m, e, a, v, out):
             quant(mq[l, g, k], turned["m", l, g, k][:].rearrange("p t f u -> p (t f u)").bitcast(BF16))
 
         def il_c(l, i, eng):
-            if i == 0:
+            if ("c", l) not in wT:
                 wT["c", l] = ring.tile([P, CH, 4], BF16, name="w_grp", tag="w_grp", bufs=2, align_bytes=64)
             dst = wT["c", l][:].rearrange("p (t q) j -> p t q j", t=4)
             src = w_t["c", l][:].rearrange("p j (q t) -> p t q j", t=4)
             copy(eng, dst[:, 2 * i : 2 * i + 2], src[:, 2 * i : 2 * i + 2])
 
         def il_e(l, i, eng):
-            if i == 0:
+            if ("e", l) not in wT:
                 wT["e", l] = ring.tile([P, CH, 4], BF16, name="w_grp", tag="w_grp", bufs=2, align_bytes=64)
-            dst = wT["e", l][:, 256 * i : 256 * i + 256, :].rearrange("p (q i) j -> p q j i", i=4)
-            src = w_t["e", l][:, :, 256 * i : 256 * i + 256].rearrange("p j (q i) -> p q j i", i=4)
-            copy(eng, dst, src)
+            dst = wT["e", l][:].rearrange("p (t q) j -> p t q j", t=4)
+            src = w_t["e", l][:].rearrange("p j (q t) -> p t q j", t=4)
+            copy(eng, dst[:, 2 * i : 2 * i + 2], src[:, 2 * i : 2 * i + 2])
 
         def qw(key, l):
             wq[key, l] = codes("%s%d" % (key, l), CH)
@@ -147,7 +151,7 @@ def tile_gait_leg_exchange_t1_kernel(tc, x, c, m, e, a, v, out):
 
         def h(l, g, *ts):
             for t in ts:
-                if t == 0:
+                if (l, g) not in h_t:
                     h_t[l, g] = keep.tile([P, 4, CH], F32, name="h%d%d" % (l, g), align_bytes=64)
                 nc.vector.scalar_tensor_tensor(
                     out=h_t[l, g][:, t, :].rearrange("p (j q) -> p j q", j=4),
@@ -159,7 +163,7 @@ def tile_gait_leg_exchange_t1_kernel(tc, x, c, m, e, a, v, out):
                 )
 
         def hb(l, g, i, eng):
-            if i == 0:
+            if (l, g) not in hT:
                 hT[l, g] = ring.tile([P, CH, 4], BF16, name="h_grp", tag="h_grp", bufs=3, align_bytes=64)
             n = CH // 2
             dst = hT[l, g][:, n * i : n * i + n, :].rearrange("p (q i) t -> p q t i", i=4)
@@ -191,7 +195,7 @@ def tile_gait_leg_exchange_t1_kernel(tc, x, c, m, e, a, v, out):
 
         def vg(l, k, i, eng="G"):
             g_, t = divmod(k, 4)
-            if i == 0:
+            if (l, k) not in vg_t:
                 vg_t[l, k] = ring.tile([P, CH], F32, name="vg", tag="vg", bufs=16, align_bytes=64)
             q = slice(64 * i, 64 * i + 64)
             (nc.vector if eng == "V" else nc.gpsimd).tensor_tensor(
@@ -203,7 +207,7 @@ def tile_gait_leg_exchange_t1_kernel(tc, x, c, m, e, a, v, out):
 
         def tg(l, k):
             g_, t = divmod(k, 4)
-            if k % 2 == 0:
+            if (l, k // 2) not in gT:
                 gT[l, k // 2] = ring.tile([P, 2, P, 4], BF16, name="g_turned", tag="g_turned", bufs=4, align_bytes=64)
             tp["g", l, k] = bank("tp")
             for j in range(4):
@@ -221,16 +225,62 @@ def tile_gait_leg_exchange_t1_kernel(tc, x, c, m, e, a, v, out):
                 o_ps[l, k] = bank("mm")
                 mx(o_ps[l, k][:], gq[1 - l, k // 2], slice(P * (k % 2), P * (k % 2) + P), wq["e", l], True, True)
 
-        def y(l, *ks):
-            for k in ks:
-                g_, t = divmod(k, 4)
-                nc.vector.tensor_tensor(out=vg_t[l, k][:], in0=o_ps[l, k][:], in1=vg_t[l, k][:], op=ADD)
-                nc.sync.dma_start(out=out_v[l, g_, t], in_=vg_t[l, k][:])
+        def y(l, k):
+            g_, t = divmod(k, 4)
+            natural = vg_t[l, k][:].rearrange("p (q j) -> p q j", j=4)
+            nc.vector.tensor_tensor(out=natural, in0=o_ps[l, k][:].rearrange("p (j q) -> p q j", j=4), in1=natural, op=ADD)
+            nc.sync.dma_start(out=out_v[l, g_, t], in_=vg_t[l, k][:])
+
+        def cgv(l, k):
+            vg_t[l, k] = ring.tile([P, CH], F32, name="vg", tag="vg", bufs=16, align_bytes=64)
+            for j in range(4):
+                nc.scalar.activation(
+                    out=vg_t[l, k][:, P * j : P * j + P],
+                    in_=tp["g", l, k][:, P * j : P * j + P],
+                    func=COPY,
+                    scale=v_f[:, 4 * l + j : 4 * l + j + 1],
+                )
+
+        def ot(l, k):
+            o_ps[l, k] = bank("mm")
+            left, cols = gq[1 - l, k // 2], slice(P * (k % 2), P * (k % 2) + P)
+            for j in range(4):
+                ch = slice(P * j, P * j + P)
+                nc.tensor.matmul_mx(
+                    out=o_ps[l, k][:, ch],
+                    lhsT=wq["e", l][0][:, ch].bitcast(FP8X4),
+                    lhsT_scale=wq["e", l][1][:, ch],
+                    rhs=left[0][:, cols].bitcast(FP8X4),
+                    rhs_scale=left[1][:, cols],
+                    start=True,
+                    stop=True,
+                )
+
+        def co(l, k, eng="S"):
+            oT[l, k] = ring.tile([P, CH], F32, name="o_t", tag="o_t", bufs=2, align_bytes=64)
+            copy(eng, oT[l, k][:], o_ps[l, k][:])
+
+        def ty(l, k):
+            tp["y", l, k] = bank("tp")
+            for j in range(4):
+                ch = slice(P * j, P * j + P)
+                for i, src in enumerate((vg_t[l, k], oT[l, k])):
+                    nc.tensor.matmul(
+                        out=tp["y", l, k][:, ch], lhsT=src[:, ch], rhs=ident[:], is_transpose=True, start=i == 0, stop=i == 1
+                    )
+
+        def yc(l, k, eng="S"):
+            g_, t = divmod(k, 4)
+            y_t = ring.tile([P, CH], F32, name="vg", tag="vg", bufs=16, align_bytes=64)
+            copy(eng, y_t[:].rearrange("p (q j) -> p q j", j=4), tp["y", l, k][:].rearrange("p (j q) -> p q j", j=4))
+            nc.sync.dma_start(out=out_v[l, g_, t], in_=y_t[:])
 
         with tc.manual_schedule():
             nc.gpsimd.dma_start(out=a_b[:], in_=a_v)
+            nc.gpsimd.dma_start(out=v_b[:], in_=v_v)
             make_identity(nc, ident[:])
             nc.gpsimd.dma_start(out=v_t[:], in_=v.rearrange("l c -> (l c)").partition_broadcast(P))
+            nc.gpsimd.tensor_copy(out=v_f[:], in_=v_b[:].rearrange("p l j -> p (l j)"))
             nc.gpsimd.tensor_copy(out=a_f[:], in_=a_b[:].rearrange("p l g t -> p (l g t)"))
             load_x(0, 0, 2)
             load_w(("c", 0), c_v[0])
@@ -251,249 +301,254 @@ def tile_gait_leg_exchange_t1_kernel(tc, x, c, m, e, a, v, out):
             il_c(0, 0, "V")
             il_c(0, 1, "V")
             tx(0, 1, 0)
-            qx(0, 0)
             tx(0, 1, 1)
+            qx(0, 0)
             cx(0, 1, 0, "S")
             qw("c", 0)
-            cx(0, 1, 1, "S")
-            z(0, 0, 0)
             il_c(1, 0, "S")
-            qx(0, 1)
-            z(0, 0, 1)
-            tx(1, 0, 0)
-            h(0, 0, 0)
-            tx(1, 0, 1)
-            h(0, 0, 1)
-            il_c(1, 1, "S")
             z(0, 0, 2)
-            z(0, 0, 3)
+            tx(1, 0, 0)
             h(0, 0, 2)
-            z(0, 1, 0)
-            cx(1, 0, 0, "S")
-            z(0, 1, 1)
-            h(0, 0, 3)
-            z(0, 1, 2)
-            cx(1, 0, 1, "S")
-            tx(1, 1, 0)
-            h(0, 1, 0)
-            z(0, 1, 3)
-            hb(0, 0, 0, "S")
-            h(0, 1, 1)
+            il_c(1, 1, "S")
+            tx(1, 0, 1)
             tx(1, 1, 1)
+            cx(1, 0, 0, "S")
             qw("c", 1)
-            hb(0, 0, 1, "S")
-            tm(0, 0, 0, 0)
-            qx(1, 0)
-            tm(0, 0, 0, 1)
-            h(0, 1, 2)
-            z(1, 0, 0)
-            cx(1, 1, 0, "S")
-            z(1, 0, 1)
-            h(0, 1, 3)
-            z(1, 0, 2)
+            z(0, 0, 1)
+            z(0, 0, 0)
             cx(1, 1, 1, "S")
-            qh(0, 0)
-            hb(0, 1, 0, "G")
-            z(1, 0, 3)
-            cm(0, 0, 0, 0)
-            tm(0, 0, 1, 0)
-            h(1, 0, 0)
-            cm(0, 0, 0, 1)
-            h(1, 0, 1)
+            h(0, 0, 1)
+            z(0, 0, 3)
+            tx(1, 1, 0)
+            cx(1, 0, 1, "S")
+            h(0, 0, 3)
             tm(0, 0, 1, 1)
-            hb(0, 1, 1, "G")
-            cm(0, 0, 1, 0)
-            tm(0, 1, 0, 0)
+            cx(0, 1, 1, "S")
+            h(0, 0, 0)
+            tm(0, 0, 1, 0)
+            cx(1, 1, 0, "S")
+            qx(0, 1)
+            tm(0, 0, 0, 1)
+            hb(0, 0, 1, "S")
             qx(1, 1)
+            z(0, 1, 1)
+            tm(0, 1, 1, 1)
+            qx(1, 0)
+            cm(0, 0, 0, 1)
+            z(1, 1, 2)
+            h(0, 1, 1)
+            z(1, 1, 1)
+            cm(0, 0, 1, 0)
+            h(1, 1, 2)
+            tm(0, 1, 1, 0)
             cm(0, 0, 1, 1)
+            h(1, 1, 1)
+            z(1, 1, 0)
+            cm(0, 1, 1, 0)
+            z(1, 1, 3)
+            qm(0, 0, 1)
+            z(0, 1, 0)
+            hb(0, 0, 0, "S")
+            z(1, 0, 2)
+            h(0, 1, 0)
             tm(0, 1, 0, 1)
             h(1, 0, 2)
-            z(1, 1, 0)
-            cm(0, 1, 0, 0)
-            h(1, 0, 3)
-            z(1, 1, 1)
-            z(1, 1, 2)
-            il_e(0, 0, "S")
-            load_w(("e", 1), e_v[1])
-            h(1, 1, 0)
-            z(1, 1, 3)
-            h(1, 1, 1)
-            tm(0, 1, 1, 0)
-            hb(1, 0, 0, "S")
-            qm(0, 0, 0)
-            tm(0, 1, 1, 1)
-            h(1, 1, 2)
-            hb(1, 0, 1, "S")
-            h(1, 1, 3)
-            qh(0, 1)
-            hb(1, 1, 0, "G")
-            tm(1, 0, 0, 0)
-            qm(0, 0, 1)
-            cm(0, 1, 0, 1)
-            cm(0, 1, 1, 0)
-            qh(1, 0)
             tm(1, 0, 0, 1)
-            r(0, 0)
-            hb(1, 1, 1, "G")
-            cm(0, 1, 1, 1)
-            r(0, 1)
-            qm(0, 1, 0)
-            r(0, 2)
-            cm(1, 0, 0, 0)
-            r(0, 3)
-            g(0, 0)
-            il_e(0, 1, "S")
-            g(0, 1)
-            vg(0, 0, 0)
-            tg(0, 0)
-            g(0, 2)
-            vg(0, 0, 1)
-            tg(0, 1)
-            g(0, 3)
-            cg(0, 0)
-            vg(0, 1, 0)
-            qm(0, 1, 1)
-            tg(0, 2)
-            cg(0, 1)
-            vg(0, 1, 1)
-            tg(0, 3)
+            cm(0, 1, 0, 1)
+            load_w(("e", 1), e_v[1])
+            qh(0, 0)
+            tm(1, 0, 0, 0)
             cm(1, 0, 0, 1)
-            qh(1, 1)
-            r(0, 4)
-            vg(0, 2, 0)
+            z(1, 0, 0)
+            h(1, 1, 0)
+            z(0, 1, 3)
+            cm(1, 0, 0, 0)
+            h(1, 1, 3)
+            tm(1, 1, 1, 1)
+            cm(0, 1, 1, 1)
+            h(0, 1, 3)
+            tm(1, 1, 0, 1)
+            hb(1, 1, 0, "S")
+            tm(1, 1, 0, 0)
+            qm(0, 1, 1)
+            z(0, 1, 2)
+            qm(1, 0, 0)
+            z(1, 0, 1)
+            cm(1, 1, 0, 1)
+            tm(1, 0, 1, 0)
+            h(0, 1, 2)
+            cm(1, 1, 0, 0)
+            tm(1, 1, 1, 0)
+            h(1, 0, 1)
+            hb(0, 1, 1, "S")
+            tm(0, 1, 0, 0)
+            qm(1, 1, 0)
+            z(1, 0, 3)
+            h(1, 0, 0)
+            cm(1, 1, 1, 0)
+            h(1, 0, 3)
+            cm(0, 1, 0, 0)
+            tm(0, 0, 0, 0)
+            hb(0, 1, 0, "S")
+            qm(0, 1, 0)
+            tm(1, 0, 1, 1)
+            cm(1, 1, 1, 1)
+            qh(0, 1)
+            cm(0, 0, 0, 0)
+            qm(1, 1, 1)
             r(0, 5)
-            cg(0, 2)
-            qg(0, 0)
-            vg(0, 2, 1)
-            g(0, 4)
-            cg(0, 3)
-            vg(0, 3, 0)
+            cm(1, 0, 1, 0)
+            qm(0, 0, 0)
+            r(0, 7)
+            hb(1, 0, 0, "S")
             g(0, 5)
             r(0, 6)
-            il_e(1, 0, "S")
-            r(0, 7)
-            qg(0, 2)
-            vg(0, 3, 1)
-            tg(0, 4)
-            g(0, 6)
-            tg(0, 5)
-            vg(0, 4, 0)
-            tm(1, 0, 1, 0)
-            cg(0, 4)
             g(0, 7)
-            vg(0, 4, 1)
-            tm(1, 0, 1, 1)
-            cg(0, 5)
-            qm(1, 0, 0)
-            vg(0, 5, 0)
-            tg(0, 6)
-            cm(1, 0, 1, 0)
-            qw("e", 0)
+            r(0, 3)
+            hb(1, 1, 1, "S")
+            r(0, 0)
+            g(0, 6)
             tg(0, 7)
-            vg(0, 5, 1)
+            vg(0, 7, 1, "V")
+            vg(0, 6, 1, "V")
+            tg(0, 6)
             cm(1, 0, 1, 1)
-            qg(0, 4)
-            tm(1, 1, 0, 0)
-            vg(0, 6, 0)
-            cg(0, 6)
-            qm(1, 0, 1)
-            tm(1, 1, 0, 1)
+            qh(1, 1)
+            r(0, 1)
             cg(0, 7)
-            vg(0, 6, 1)
-            r(1, 0)
-            cm(1, 1, 0, 0)
-            vg(0, 7, 0)
-            qg(0, 6)
-            g(1, 0)
-            tm(1, 1, 1, 0)
-            cm(1, 1, 0, 1)
-            vg(0, 7, 1)
-            r(1, 1)
-            il_e(1, 1, "S")
-            tg(1, 0)
-            qm(1, 1, 0)
-            vg(1, 0, 0)
-            g(1, 1)
-            vg(1, 0, 1)
-            tm(1, 1, 1, 1)
-            cg(1, 0)
-            qw("e", 1)
-            vg(1, 1, 0)
-            tg(1, 1)
-            cm(1, 1, 1, 0)
-            vg(1, 1, 1)
-            cg(1, 1)
-            r(1, 2)
-            r(1, 3)
-            g(1, 2)
-            cm(1, 1, 1, 1)
-            o(1, 0)
-            o(1, 1)
-            g(1, 3)
-            vg(1, 2, 0)
-            tg(1, 2)
-            qm(1, 1, 1)
-            vg(1, 2, 1)
-            cg(1, 2)
-            tg(1, 3)
-            qg(1, 0)
-            vg(1, 3, 0)
+            qm(1, 0, 1)
+            r(0, 2)
+            cg(0, 6)
+            tg(0, 5)
+            g(0, 3)
+            hb(1, 0, 1, "S")
+            g(0, 2)
+            tg(0, 3)
+            r(0, 4)
+            vg(0, 7, 0, "V")
+            g(0, 0)
+            cg(0, 3)
+            tg(0, 2)
+            g(0, 4)
+            tg(0, 0)
+            cgv(0, 3)
+            qh(1, 0)
+            cg(0, 2)
+            tg(0, 4)
+            vg(0, 5, 0, "V")
+            r(1, 7)
+            cgv(0, 2)
+            qg(0, 2)
+            g(0, 1)
             r(1, 4)
+            cgv(0, 4)
+            g(1, 7)
+            r(1, 6)
+            cg(0, 4)
+            g(1, 4)
+            r(1, 2)
+            cg(0, 5)
+            tg(1, 7)
+            g(1, 6)
+            cg(0, 0)
+            r(1, 5)
+            qg(0, 4)
+            cg(1, 7)
+            vg(1, 6, 0, "V")
+            tg(1, 6)
+            vg(1, 4, 1, "V")
+            il_e(0, 1, "S")
+            r(1, 3)
+            vg(1, 4, 0, "V")
+            g(1, 5)
+            r(1, 1)
+            g(1, 3)
+            il_e(1, 1, "S")
+            tg(1, 5)
+            g(1, 1)
+            r(1, 0)
+            vg(1, 5, 1, "V")
+            tg(1, 1)
+            cg(1, 5)
+            vg(1, 1, 1, "V")
+            g(1, 0)
+            cg(1, 6)
+            tg(1, 3)
+            vg(1, 3, 0, "V")
+            il_e(0, 0, "S")
+            tg(1, 0)
+            qg(1, 6)
+            vg(1, 0, 1, "V")
+            vg(1, 5, 0, "V")
+            g(1, 2)
+            cg(1, 1)
+            qw("e", 0)
+            cg(1, 0)
+            tg(1, 2)
+            vg(1, 7, 1, "V")
+            il_e(1, 0, "S")
+            o(0, 7)
+            qg(1, 0)
+            o(0, 6)
+            vg(1, 3, 1, "V")
+            ot(0, 0)
+            y(0, 7)
+            ot(0, 1)
+            cg(1, 2)
+            tg(1, 4)
+            qw("e", 1)
+            co(0, 1)
+            tg(0, 1)
+            vg(1, 2, 0, "V")
+            o(1, 4)
+            cg(1, 4)
+            vg(1, 7, 0, "V")
+            o(1, 5)
+            vg(1, 2, 1, "V")
+            cg(0, 1)
+            y(1, 4)
+            cgv(0, 1)
+            qg(1, 4)
+            o(1, 3)
+            qg(0, 0)
+            co(0, 0)
+            ty(0, 1)
+            y(1, 3)
+            cgv(0, 0)
+            y(1, 5)
+            ot(0, 4)
+            yc(0, 1)
+            o(1, 0)
+            vg(1, 0, 0, "V")
+            o(1, 2)
+            vg(0, 6, 0, "V")
+            ty(0, 0)
+            co(0, 4)
             y(1, 0)
             cg(1, 3)
-            vg(1, 3, 1)
-            y(1, 1)
-            r(1, 5)
-            o(0, 0)
-            g(1, 4)
-            o(0, 1)
-            g(1, 5)
-            tg(1, 4)
-            vg(1, 4, 0)
-            o(1, 2)
-            qg(1, 2)
-            cg(1, 4)
-            vg(1, 4, 1)
-            y(0, 0)
-            tg(1, 5)
-            vg(1, 5, 0)
-            o(1, 3)
-            y(0, 1)
-            cg(1, 5)
-            vg(1, 5, 1)
-            y(1, 2)
-            r(1, 6)
-            y(1, 3)
-            o(0, 2)
-            r(1, 7)
-            g(1, 6)
-            o(0, 3)
-            g(1, 7)
-            tg(1, 6)
-            vg(1, 6, 0)
-            o(1, 4)
-            qg(1, 4)
-            cg(1, 6)
-            vg(1, 6, 1)
-            y(0, 2)
-            tg(1, 7)
-            vg(1, 7, 0)
-            o(1, 5)
-            y(0, 3)
-            cg(1, 7)
-            o(0, 4)
-            vg(1, 7, 1)
-            y(1, 4)
-            o(0, 5)
-            y(1, 5)
-            o(1, 6)
-            qg(1, 6)
-            o(1, 7)
-            y(0, 4)
-            y(0, 5)
-            o(0, 6)
-            y(1, 6)
-            o(0, 7)
-            y(1, 7)
             y(0, 6)
-            y(0, 7)
+            ty(0, 4)
+            yc(0, 0)
+            qg(1, 2)
+            o(0, 5)
+            y(1, 2)
+            yc(0, 4)
+            ot(0, 2)
+            ot(0, 3)
+            vg(1, 1, 0, "V")
+            co(0, 2)
+            o(1, 1)
+            vg(0, 5, 1, "V")
+            y(1, 1)
+            co(0, 3)
+            ty(0, 2)
+            y(0, 5)
+            ty(0, 3)
+            yc(0, 2)
+            qg(0, 6)
+            vg(1, 6, 1, "V")
+            o(1, 7)
+            yc(0, 3)
+            o(1, 6)
+            y(1, 7)
+            y(1, 6)

@@ -138,7 +138,7 @@ def tile_gait_leg_exchange_t1_kernel(tc, x, c, m, e, a, v, out):
                 wT["e", l] = ring.tile([P, CH, 4], BF16, name="w_grp", tag="w_grp", bufs=2, align_bytes=64)
             dst = wT["e", l][:].rearrange("p (t q) j -> p t q j", t=4)
             src = w_t["e", l][:].rearrange("p j (q t) -> p t q j", t=4)
-            copy(eng, dst[:, 2 * i : 2 * i + 2], src[:, 2 * i : 2 * i + 2])
+            copy(eng, dst[:, 1 * i : 1 * i + 1], src[:, 1 * i : 1 * i + 1])
 
         def qw(key, l):
             wq[key, l] = codes("%s%d" % (key, l), CH)
@@ -148,6 +148,9 @@ def tile_gait_leg_exchange_t1_kernel(tc, x, c, m, e, a, v, out):
             for t in ts:
                 z_ps[l, g, t] = bank("mm")
                 mx(z_ps[l, g, t][:], xq[l, g], slice(P * t, P * t + P), wq["c", l], True, True)
+
+        def dm(l, g, i):
+            mx(bank("mm")[:], xq[l, g], slice(P * (i % 4), P * (i % 4) + P), wq["c", l], True, True)
 
         def h(l, g, *ts):
             for t in ts:
@@ -165,7 +168,7 @@ def tile_gait_leg_exchange_t1_kernel(tc, x, c, m, e, a, v, out):
         def hb(l, g, i, eng):
             if (l, g) not in hT:
                 hT[l, g] = ring.tile([P, CH, 4], BF16, name="h_grp", tag="h_grp", bufs=3, align_bytes=64)
-            n = CH // 2
+            n = CH // 4
             dst = hT[l, g][:, n * i : n * i + n, :].rearrange("p (q i) t -> p q t i", i=4)
             src = h_t[l, g][:, :, n * i : n * i + n].rearrange("p t (q i) -> p q t i", i=4)
             copy(eng, dst, src)
@@ -275,280 +278,298 @@ def tile_gait_leg_exchange_t1_kernel(tc, x, c, m, e, a, v, out):
             copy(eng, y_t[:].rearrange("p (q j) -> p q j", j=4), tp["y", l, k][:].rearrange("p (j q) -> p q j", j=4))
             nc.sync.dma_start(out=out_v[l, g_, t], in_=y_t[:])
 
-        with tc.manual_schedule():
-            nc.gpsimd.dma_start(out=a_b[:], in_=a_v)
-            nc.gpsimd.dma_start(out=v_b[:], in_=v_v)
-            make_identity(nc, ident[:])
-            nc.gpsimd.dma_start(out=v_t[:], in_=v.rearrange("l c -> (l c)").partition_broadcast(P))
-            nc.gpsimd.tensor_copy(out=v_f[:], in_=v_b[:].rearrange("p l j -> p (l j)"))
+        def load_small():
+            nc.sync.dma_start(out=a_b[:], in_=a_v)
+            nc.sync.dma_start(out=v_b[:], in_=v_v)
             nc.gpsimd.tensor_copy(out=a_f[:], in_=a_b[:].rearrange("p l g t -> p (l g t)"))
+            nc.gpsimd.tensor_copy(out=v_f[:], in_=v_b[:].rearrange("p l j -> p (l j)"))
+
+        def load_v():
+            nc.sync.dma_start(out=v_t[:], in_=v.rearrange("l c -> (l c)").partition_broadcast(P))
+
+        with tc.manual_schedule():
+            make_identity(nc, ident[:])
             load_x(0, 0, 2)
             load_w(("c", 0), c_v[0])
             load_x(0, 1)
+            load_m(0, 0)
             load_w(("c", 1), c_v[1])
             load_x(1, 0)
-            load_x(1, 1)
-            load_m(0, 0)
             load_m(0, 1)
+            load_small()
+            load_x(1, 1)
             load_w(("e", 0), e_v[0])
             load_m(1, 0)
             load_m(1, 1)
-
+            load_v()
             tx(0, 0, 0)
             tx(0, 0, 1)
             cx(0, 0, 0, "S")
-            cx(0, 0, 1, "V")
-            il_c(0, 0, "V")
             il_c(0, 1, "V")
-            tx(0, 1, 0)
+            cx(0, 0, 1, "V")
             tx(0, 1, 1)
+            il_c(0, 0, "V")
             qx(0, 0)
-            cx(0, 1, 0, "S")
-            qw("c", 0)
-            il_c(1, 0, "S")
-            z(0, 0, 2)
-            tx(1, 0, 0)
-            h(0, 0, 2)
-            il_c(1, 1, "S")
-            tx(1, 0, 1)
-            tx(1, 1, 1)
-            cx(1, 0, 0, "S")
-            qw("c", 1)
-            z(0, 0, 1)
-            z(0, 0, 0)
-            cx(1, 1, 1, "S")
-            h(0, 0, 1)
-            z(0, 0, 3)
-            tx(1, 1, 0)
-            cx(1, 0, 1, "S")
-            h(0, 0, 3)
-            tm(0, 0, 1, 1)
+            tx(0, 1, 0)
             cx(0, 1, 1, "S")
-            h(0, 0, 0)
-            tm(0, 0, 1, 0)
-            cx(1, 1, 0, "S")
-            qx(0, 1)
+            qw("c", 0)
             tm(0, 0, 0, 1)
-            hb(0, 0, 1, "S")
-            qx(1, 1)
-            z(0, 1, 1)
-            tm(0, 1, 1, 1)
-            qx(1, 0)
+            cx(0, 1, 0, "S")
+            qx(0, 1)
+            z(0, 0, 2)
+            il_c(1, 0, "S")
+            z(0, 1, 2)
+            h(0, 0, 2)
+            z(0, 1, 0)
             cm(0, 0, 0, 1)
-            z(1, 1, 2)
+            h(0, 1, 2)
+            z(0, 0, 0)
+            il_c(1, 1, "S")
+            z(0, 1, 3)
+            h(0, 0, 0)
+            tm(0, 0, 0, 0)
+            h(0, 1, 0)
+            tx(1, 0, 1)
+            cm(0, 0, 0, 0)
+            tm(0, 1, 0, 0)
+            qw("c", 1)
+            cx(1, 0, 1, "S")
+            z(0, 0, 3)
+            qm(0, 0, 0)
+            cm(0, 1, 0, 0)
+            z(0, 1, 1)
+            tm(0, 0, 1, 1)
             h(0, 1, 1)
-            z(1, 1, 1)
-            cm(0, 0, 1, 0)
-            h(1, 1, 2)
-            tm(0, 1, 1, 0)
+            tx(1, 0, 0)
+            il_e(0, 3, "G")
             cm(0, 0, 1, 1)
-            h(1, 1, 1)
+            h(0, 0, 3)
+            tm(0, 1, 0, 1)
+            cx(1, 0, 0, "S")
+            il_e(0, 0, "G")
+            h(0, 1, 3)
+            tx(1, 1, 0)
+            cm(0, 1, 0, 1)
+            tm(0, 0, 1, 0)
+            qx(1, 0)
+            cx(1, 1, 0, "S")
+            z(0, 0, 1)
+            qm(0, 1, 0)
+            z(1, 0, 3)
+            hb(0, 1, 1, "S")
+            h(0, 0, 1)
+            il_e(0, 2, "G")
+            z(1, 0, 2)
+            cm(0, 0, 1, 0)
+            h(1, 0, 3)
+            il_e(0, 1, "G")
+            tm(1, 0, 1, 0)
+            load_w(("e", 1), e_v[1])
+            hb(0, 1, 0, "S")
+            h(1, 0, 2)
+            hb(0, 0, 3, "G")
+            hb(0, 1, 3, "S")
+            z(1, 0, 0)
+            qw("e", 0)
+            z(1, 0, 1)
+            cm(1, 0, 1, 0)
+            tx(1, 1, 1)
+            hb(0, 0, 0, "G")
+            h(1, 0, 0)
+            hb(0, 1, 2, "S")
+            tm(0, 1, 1, 0)
+            h(1, 0, 1)
+            hb(0, 0, 2, "G")
+            tm(1, 1, 0, 1)
+            cx(1, 1, 1, "S")
+            qh(0, 1)
+            tm(1, 0, 1, 1)
+            hb(1, 0, 1, "S")
+            tm(0, 1, 1, 1)
+            qx(1, 1)
+            hb(1, 0, 2, "S")
+            qm(0, 0, 1)
+            z(1, 1, 2)
+            hb(1, 0, 3, "S")
+            z(1, 1, 3)
+            il_e(1, 2, "G")
+            h(1, 1, 2)
+            z(1, 1, 1)
+            cm(1, 0, 1, 1)
+            hb(0, 0, 1, "G")
+            h(1, 1, 3)
             z(1, 1, 0)
             cm(0, 1, 1, 0)
-            z(1, 1, 3)
-            qm(0, 0, 1)
-            z(0, 1, 0)
-            hb(0, 0, 0, "S")
-            z(1, 0, 2)
-            h(0, 1, 0)
-            tm(0, 1, 0, 1)
-            h(1, 0, 2)
-            tm(1, 0, 0, 1)
-            cm(0, 1, 0, 1)
-            load_w(("e", 1), e_v[1])
-            qh(0, 0)
-            tm(1, 0, 0, 0)
-            cm(1, 0, 0, 1)
-            z(1, 0, 0)
-            h(1, 1, 0)
-            z(0, 1, 3)
-            cm(1, 0, 0, 0)
-            h(1, 1, 3)
-            tm(1, 1, 1, 1)
-            cm(0, 1, 1, 1)
-            h(0, 1, 3)
-            tm(1, 1, 0, 1)
-            hb(1, 1, 0, "S")
-            tm(1, 1, 0, 0)
-            qm(0, 1, 1)
-            z(0, 1, 2)
-            qm(1, 0, 0)
-            z(1, 0, 1)
-            cm(1, 1, 0, 1)
-            tm(1, 0, 1, 0)
-            h(0, 1, 2)
-            cm(1, 1, 0, 0)
+            il_e(1, 3, "G")
+            h(1, 1, 1)
             tm(1, 1, 1, 0)
-            h(1, 0, 1)
-            hb(0, 1, 1, "S")
-            tm(0, 1, 0, 0)
-            qm(1, 1, 0)
-            z(1, 0, 3)
-            h(1, 0, 0)
-            cm(1, 1, 1, 0)
-            h(1, 0, 3)
-            cm(0, 1, 0, 0)
-            tm(0, 0, 0, 0)
-            hb(0, 1, 0, "S")
-            qm(0, 1, 0)
-            tm(1, 0, 1, 1)
-            cm(1, 1, 1, 1)
-            qh(0, 1)
-            cm(0, 0, 0, 0)
-            qm(1, 1, 1)
-            r(0, 5)
-            cm(1, 0, 1, 0)
-            qm(0, 0, 0)
-            r(0, 7)
             hb(1, 0, 0, "S")
-            g(0, 5)
-            r(0, 6)
-            g(0, 7)
-            r(0, 3)
-            hb(1, 1, 1, "S")
-            r(0, 0)
-            g(0, 6)
-            tg(0, 7)
-            vg(0, 7, 1, "V")
-            vg(0, 6, 1, "V")
-            tg(0, 6)
-            cm(1, 0, 1, 1)
-            qh(1, 1)
+            h(1, 1, 0)
+            il_e(1, 0, "G")
+            cm(0, 1, 1, 1)
+            tm(1, 0, 0, 0)
+            qh(0, 0)
+            cm(1, 1, 1, 0)
+            tm(1, 0, 0, 1)
+            qm(0, 1, 1)
+            hb(1, 1, 2, "S")
             r(0, 1)
-            cg(0, 7)
             qm(1, 0, 1)
-            r(0, 2)
-            cg(0, 6)
-            tg(0, 5)
-            g(0, 3)
-            hb(1, 0, 1, "S")
-            g(0, 2)
-            tg(0, 3)
-            r(0, 4)
-            vg(0, 7, 0, "V")
-            g(0, 0)
-            cg(0, 3)
-            tg(0, 2)
-            g(0, 4)
-            tg(0, 0)
-            cgv(0, 3)
-            qh(1, 0)
-            cg(0, 2)
-            tg(0, 4)
-            vg(0, 5, 0, "V")
-            r(1, 7)
-            cgv(0, 2)
-            qg(0, 2)
+            cm(1, 0, 0, 1)
+            r(0, 7)
             g(0, 1)
-            r(1, 4)
-            cgv(0, 4)
-            g(1, 7)
-            r(1, 6)
-            cg(0, 4)
-            g(1, 4)
-            r(1, 2)
-            cg(0, 5)
-            tg(1, 7)
-            g(1, 6)
-            cg(0, 0)
-            r(1, 5)
-            qg(0, 4)
-            cg(1, 7)
-            vg(1, 6, 0, "V")
-            tg(1, 6)
-            vg(1, 4, 1, "V")
-            il_e(0, 1, "S")
-            r(1, 3)
-            vg(1, 4, 0, "V")
-            g(1, 5)
-            r(1, 1)
-            g(1, 3)
-            il_e(1, 1, "S")
-            tg(1, 5)
-            g(1, 1)
+            il_e(1, 1, "G")
+            cm(1, 0, 0, 0)
+            qh(1, 0)
+            r(0, 5)
+            cm(1, 1, 0, 1)
+            g(0, 7)
+            hb(1, 1, 0, "S")
+            r(0, 2)
+            qm(1, 0, 0)
+            hb(1, 1, 1, "S")
+            r(0, 3)
+            vg(0, 7, 0, "V")
+            hb(1, 1, 3, "S")
+            tm(1, 1, 0, 0)
+            qw("e", 1)
+            g(0, 5)
+            tg(0, 7)
+            cm(1, 1, 0, 0)
+            r(0, 6)
+            qh(1, 1)
+            cg(0, 7)
+            r(0, 4)
+            qm(1, 1, 0)
+            tg(0, 5)
+            g(0, 2)
+            tg(0, 1)
+            cgv(0, 5)
+            tm(1, 1, 1, 1)
+            g(0, 6)
             r(1, 0)
-            vg(1, 5, 1, "V")
-            tg(1, 1)
-            cg(1, 5)
-            vg(1, 1, 1, "V")
+            cg(0, 1)
+            g(0, 3)
+            cm(1, 1, 1, 1)
+            tg(0, 6)
+            vg(0, 6, 0, "V")
+            r(1, 3)
             g(1, 0)
-            cg(1, 6)
-            tg(1, 3)
-            vg(1, 3, 0, "V")
-            il_e(0, 0, "S")
+            cg(0, 5)
+            qm(1, 1, 1)
+            tg(0, 2)
+            cg(0, 6)
             tg(1, 0)
-            qg(1, 6)
-            vg(1, 0, 1, "V")
-            vg(1, 5, 0, "V")
-            g(1, 2)
-            cg(1, 1)
-            qw("e", 0)
-            cg(1, 0)
-            tg(1, 2)
-            vg(1, 7, 1, "V")
-            il_e(1, 0, "S")
-            o(0, 7)
-            qg(1, 0)
-            o(0, 6)
+            cgv(0, 1)
+            vg(1, 0, 0, "V")
+            r(0, 0)
+            g(1, 3)
+            cgv(0, 2)
+            tg(0, 3)
+            qg(0, 6)
+            tg(1, 3)
+            cg(0, 2)
+            g(0, 0)
+            r(1, 6)
+            cgv(0, 3)
             vg(1, 3, 1, "V")
-            ot(0, 0)
-            y(0, 7)
-            ot(0, 1)
+            tg(0, 0)
+            vg(1, 0, 1, "V")
+            cg(1, 3)
+            g(0, 4)
+            r(1, 2)
+            cg(0, 0)
+            g(1, 6)
+            r(1, 4)
+            cgv(0, 0)
+            g(1, 2)
+            r(1, 1)
+            cg(0, 3)
+            qg(0, 0)
+            tg(1, 6)
+            g(1, 1)
+            o(1, 0)
+            cg(1, 0)
+            o(1, 1)
+            vg(1, 2, 1, "V")
+            tg(1, 1)
+            qg(0, 2)
+            tg(1, 2)
+            g(1, 4)
+            cg(1, 1)
+            r(1, 5)
+            vg(1, 1, 0, "V")
             cg(1, 2)
             tg(1, 4)
-            qw("e", 1)
-            co(0, 1)
-            tg(0, 1)
-            vg(1, 2, 0, "V")
-            o(1, 4)
+            qg(1, 0)
+            cg(1, 6)
+            vg(1, 4, 1, "V")
+            tg(0, 4)
+            ot(0, 0)
+            y(1, 0)
             cg(1, 4)
-            vg(1, 7, 0, "V")
-            o(1, 5)
-            vg(1, 2, 1, "V")
-            cg(0, 1)
-            y(1, 4)
-            cgv(0, 1)
-            qg(1, 4)
-            o(1, 3)
-            qg(0, 0)
+            vg(1, 4, 0, "V")
+            ot(0, 1)
             co(0, 0)
+            g(1, 5)
+            co(0, 1)
+            ty(0, 0)
+            qg(1, 2)
+            vg(1, 5, 0, "V")
+            cg(0, 4)
+            tg(1, 5)
+            vg(1, 5, 1, "V")
+            yc(0, 0)
+            ot(0, 3)
+            vg(1, 6, 0, "V")
+            r(1, 7)
+            qg(0, 4)
+            cg(1, 5)
+            vg(1, 6, 1, "V")
+            o(1, 6)
+            g(1, 7)
+            co(0, 3)
             ty(0, 1)
-            y(1, 3)
-            cgv(0, 0)
+            qg(1, 4)
+            cgv(0, 4)
+            ty(0, 3)
+            y(1, 6)
+            yc(0, 1)
+            ot(0, 5)
+            vg(1, 1, 1, "V")
+            yc(0, 3)
+            o(1, 5)
+            vg(1, 7, 1, "V")
+            tg(1, 7)
+            y(1, 1)
+            co(0, 5)
+            o(1, 4)
             y(1, 5)
             ot(0, 4)
-            yc(0, 1)
-            o(1, 0)
-            vg(1, 0, 0, "V")
-            o(1, 2)
-            vg(0, 6, 0, "V")
-            ty(0, 0)
+            cg(1, 7)
+            ty(0, 5)
+            vg(1, 3, 0, "V")
             co(0, 4)
-            y(1, 0)
-            cg(1, 3)
-            y(0, 6)
-            ty(0, 4)
-            yc(0, 0)
-            qg(1, 2)
-            o(0, 5)
-            y(1, 2)
-            yc(0, 4)
+            vg(1, 2, 0, "V")
+            o(1, 2)
+            y(1, 4)
+            yc(0, 5)
             ot(0, 2)
-            ot(0, 3)
-            vg(1, 1, 0, "V")
+            o(1, 3)
+            y(1, 2)
             co(0, 2)
-            o(1, 1)
-            vg(0, 5, 1, "V")
-            y(1, 1)
-            co(0, 3)
+            ty(0, 4)
+            y(1, 3)
             ty(0, 2)
-            y(0, 5)
-            ty(0, 3)
-            yc(0, 2)
-            qg(0, 6)
-            vg(1, 6, 1, "V")
+            vg(0, 7, 1, "V")
+            yc(0, 4)
+            qg(1, 6)
             o(1, 7)
-            yc(0, 3)
-            o(1, 6)
+            yc(0, 2)
+            vg(0, 6, 1, "V")
+            o(0, 7)
+            vg(1, 7, 0, "V")
+            o(0, 6)
+            y(0, 7)
             y(1, 7)
-            y(1, 6)
+            y(0, 6)

from contextlib import ExitStack

import concourse.mybir as mybir
from concourse.masks import make_identity

LEGS, FRAMES, CH = 2, 1024, 512
FLOPS = 2 * LEGS * FRAMES * CH * (CH + FRAMES + CH)

F32 = mybir.dt.float32
BF16 = mybir.dt.bfloat16
U32 = mybir.dt.uint32
U8 = mybir.dt.uint8
FP8X4 = mybir.dt.float8_e4m3fn_x4
ADD = mybir.AluOpType.add
MULT = mybir.AluOpType.mult
MAX = mybir.AluOpType.max
COPY = mybir.ActivationFunctionType.Copy

P = 128


def tile_gait_leg_exchange_t1_kernel(tc, x, c, m, e, a, v, out):
    nc = tc.nc
    x_v = x.rearrange("l (g p t) c -> l g p t c", p=P, t=4)
    m_v = m.rearrange("l (g p t) i -> l g p t i", p=P, t=4)
    c_v = c.rearrange("l (p j) o -> l p j o", j=4)
    e_v = e.rearrange("l (p j) o -> l p j o", j=4)
    a_v = a.rearrange("l (g p t) -> p l g t", p=P, t=4)
    v_v = v.rearrange("l (p j) -> p l j", j=4)
    out_v = out.rearrange("l (g p t) c -> l g t p c", p=P, t=4)

    with ExitStack() as ctx:
        keep = ctx.enter_context(tc.tile_pool(name="keep", bufs=1))
        ring = ctx.enter_context(tc.tile_pool(name="ring", bufs=4))
        tp_pool = ctx.enter_context(tc.psum_pool(name="tp_pool", bufs=4))
        mm_pool = ctx.enter_context(tc.psum_pool(name="mm_pool", bufs=4))

        def codes(name, width):
            words = keep.tile([P, width], U32, name=name + "_codes", align_bytes=64)
            scales = keep.tile([P, width], U8, name=name + "_scales", align_bytes=64)
            return words, scales

        ident = keep.tile([P, P], F32, name="ident", align_bytes=64)
        a_b = keep.tile([P, LEGS, 2, 4], BF16, name="a_b", align_bytes=64)
        a_f = keep.tile([P, LEGS * 8], F32, name="a_f", align_bytes=64)
        v_t = keep.tile([P, LEGS, CH], BF16, name="v_t", align_bytes=64)
        v_b = keep.tile([P, LEGS, 4], BF16, name="v_b", align_bytes=64)
        v_f = keep.tile([P, LEGS * 4], F32, name="v_f", align_bytes=64)
        x_t, m_t, w_t, h_t = {}, {}, {}, {}
        xq, mq, wq, hq, gq = {}, {}, {}, {}, {}
        turned, tp, wT, hT, gT, vg_t, oT = {}, {}, {}, {}, {}, {}, {}
        z_ps, r_ps, o_ps = {}, {}, {}

        def load_x(l, g, parts=1):
            x_t[l, g] = keep.tile([P, 4, CH], BF16, name="x%d%d" % (l, g), align_bytes=64)
            n = 4 // parts
            for i in range(parts):
                nc.sync.dma_start(out=x_t[l, g][:, n * i : n * i + n, :], in_=x_v[l, g][:, n * i : n * i + n, :])

        def load_m(l, g):
            m_t[l, g] = ring.tile([P, 4, FRAMES], BF16, name="m_raw", tag="m_raw", bufs=4, align_bytes=64)
            nc.sync.dma_start(out=m_t[l, g][:], in_=m_v[l, g])

        def load_w(key, src):
            w_t[key] = ring.tile([P, 4, CH], BF16, name="w_raw", tag="w_raw", bufs=3, align_bytes=64)
            nc.sync.dma_start(out=w_t[key][:], in_=src)

        def mx(dst, left, lcols, right, start, stop):
            nc.tensor.matmul_mx(
                out=dst,
                lhsT=left[0][:, lcols].bitcast(FP8X4),
                lhsT_scale=left[1][:, lcols],
                rhs=right[0][:].bitcast(FP8X4),
                rhs_scale=right[1][:],
                start=start,
                stop=stop,
            )

        def quant(dst, src):
            nc.vector.quantize_mx(out=dst[0][:].bitcast(FP8X4), scales=dst[1][:], in_=src)

        def bank(kind):
            if kind == "tp":
                return tp_pool.tile([P, CH], F32, name="tp", tag="tp")
            return mm_pool.tile([P, CH], F32, name="mm", tag="mm")

        def copy(eng, dst, src):
            if eng == "S":
                nc.scalar.copy(out=dst, in_=src)
            elif eng == "V":
                nc.vector.tensor_copy(out=dst, in_=src)
            else:
                nc.gpsimd.tensor_scalar(out=dst, in0=src, scalar1=1.0, scalar2=0.0, op0=MULT, op1=ADD)

        def turn(key, src, base, half):
            words = src[:].rearrange("p t k -> p (t k)").bitcast(F32).rearrange("p (t k) -> p t k", t=4)
            if key not in turned:
                turned[key] = ring.tile([P, 4, P, 2], F32, name="turned", tag="turned", bufs=4, align_bytes=64)
            tp[key, half] = bank("tp")
            ps4 = tp[key, half][:].rearrange("p (t u f) -> p t u f", t=2, u=2)
            for i in range(2):
                for u in range(2):
                    nc.tensor.transpose(ps4[:, i, u, :], words[:, 2 * half + i, base + u : base + 256 : 2], ident[:])

        def turnc(key, half, eng):
            ps4 = tp[key, half][:].rearrange("p (t u f) -> p t u f", t=2, u=2)
            copy(eng, turned[key][:, 2 * half : 2 * half + 2, :, :], ps4.rearrange("p t u f -> p t f u"))

        def tx(l, g, half):
            turn(("x", l, g), x_t[l, g], 0, half)

        def cx(l, g, half, eng="S"):
            turnc(("x", l, g), half, eng)

        def tm(l, g, k, half):
            turn(("m", l, g, k), m_t[l, g], 256 * k, half)

        def cm(l, g, k, half, eng="S"):
            turnc(("m", l, g, k), half, eng)

        def qx(l, g):
            xq[l, g] = codes("x%d%d" % (l, g), CH)
            quant(xq[l, g], turned["x", l, g][:].rearrange("p t f u -> p (t f u)").bitcast(BF16))

        def qm(l, g, k):
            mq[l, g, k] = codes("m%d%d%d" % (l, g, k), CH)
            quant(mq[l, g, k], turned["m", l, g, k][:].rearrange("p t f u -> p (t f u)").bitcast(BF16))

        def il_c(l, i, eng):
            if ("c", l) not in wT:
                wT["c", l] = ring.tile([P, CH, 4], BF16, name="w_grp", tag="w_grp", bufs=2, align_bytes=64)
            dst = wT["c", l][:].rearrange("p (t q) j -> p t q j", t=4)
            src = w_t["c", l][:].rearrange("p j (q t) -> p t q j", t=4)
            copy(eng, dst[:, 2 * i : 2 * i + 2], src[:, 2 * i : 2 * i + 2])

        def il_e(l, i, eng):
            if ("e", l) not in wT:
                wT["e", l] = ring.tile([P, CH, 4], BF16, name="w_grp", tag="w_grp", bufs=2, align_bytes=64)
            dst = wT["e", l][:].rearrange("p (t q) j -> p t q j", t=4)
            src = w_t["e", l][:].rearrange("p j (q t) -> p t q j", t=4)
            copy(eng, dst[:, 1 * i : 1 * i + 1], src[:, 1 * i : 1 * i + 1])

        def qw(key, l):
            wq[key, l] = codes("%s%d" % (key, l), CH)
            quant(wq[key, l], wT[key, l][:].rearrange("p o j -> p (o j)"))

        def z(l, g, *ts):
            for t in ts:
                z_ps[l, g, t] = bank("mm")
                mx(z_ps[l, g, t][:], xq[l, g], slice(P * t, P * t + P), wq["c", l], True, True)

        def dm(l, g, i):
            mx(bank("mm")[:], xq[l, g], slice(P * (i % 4), P * (i % 4) + P), wq["c", l], True, True)

        def h(l, g, *ts):
            for t in ts:
                if (l, g) not in h_t:
                    h_t[l, g] = keep.tile([P, 4, CH], F32, name="h%d%d" % (l, g), align_bytes=64)
                nc.vector.scalar_tensor_tensor(
                    out=h_t[l, g][:, t, :].rearrange("p (j q) -> p j q", j=4),
                    in0=z_ps[l, g, t][:].rearrange("p (j q) -> p j q", j=4),
                    scalar=0.0,
                    in1=x_t[l, g][:, t, :].rearrange("p (q j) -> p j q", j=4),
                    op0=MAX,
                    op1=ADD,
                )

        def hb(l, g, i, eng):
            if (l, g) not in hT:
                hT[l, g] = ring.tile([P, CH, 4], BF16, name="h_grp", tag="h_grp", bufs=3, align_bytes=64)
            n = CH // 4
            dst = hT[l, g][:, n * i : n * i + n, :].rearrange("p (q i) t -> p q t i", i=4)
            src = h_t[l, g][:, :, n * i : n * i + n].rearrange("p t (q i) -> p q t i", i=4)
            copy(eng, dst, src)

        def qh(l, g):
            hq[l, g] = codes("h%d%d" % (l, g), CH)
            quant(hq[l, g], hT[l, g][:].rearrange("p o t -> p (o t)"))

        def r(l, *ks):
            for k in ks:
                g_, t = divmod(k, 4)
                r_ps[l, k] = bank("mm")
                for kk in range(2):
                    mx(r_ps[l, k][:], mq[l, g_, kk], slice(P * t, P * t + P), hq[l, kk], kk == 0, kk == 1)

        def g(l, *ks):
            for k in ks:
                g_, t = divmod(k, 4)
                nc.vector.scalar_tensor_tensor(
                    out=h_t[l, g_][:, t, :],
                    in0=h_t[l, g_][:, t, :],
                    scalar=a_f[:, 8 * l + k : 8 * l + k + 1],
                    in1=r_ps[l, k][:],
                    op0=MULT,
                    op1=ADD,
                )

        def vg(l, k, i, eng="G"):
            g_, t = divmod(k, 4)
            if (l, k) not in vg_t:
                vg_t[l, k] = ring.tile([P, CH], F32, name="vg", tag="vg", bufs=16, align_bytes=64)
            q = slice(64 * i, 64 * i + 64)
            (nc.vector if eng == "V" else nc.gpsimd).tensor_tensor(
                out=vg_t[l, k][:].rearrange("p (q j) -> p q j", j=4)[:, q, :],
                in0=h_t[l, g_][:, t, :].rearrange("p (j q) -> p q j", j=4)[:, q, :],
                in1=v_t[:, l, :].rearrange("p (q j) -> p q j", j=4)[:, q, :],
                op=MULT,
            )

        def tg(l, k):
            g_, t = divmod(k, 4)
            if (l, k // 2) not in gT:
                gT[l, k // 2] = ring.tile([P, 2, P, 4], BF16, name="g_turned", tag="g_turned", bufs=4, align_bytes=64)
            tp["g", l, k] = bank("tp")
            for j in range(4):
                nc.tensor.transpose(tp["g", l, k][:, P * j : P * j + P], h_t[l, g_][:, t, P * j : P * j + P], ident[:])

        def cg(l, k):
            nc.scalar.copy(out=gT[l, k // 2][:, k % 2], in_=tp["g", l, k][:].rearrange("p (j f) -> p f j", j=4))

        def qg(l, k):
            gq[l, k // 2] = codes("g%d%d" % (l, k // 2), 2 * P)
            quant(gq[l, k // 2], gT[l, k // 2][:].rearrange("p i f j -> p (i f j)"))

        def o(l, *ks):
            for k in ks:
                o_ps[l, k] = bank("mm")
                mx(o_ps[l, k][:], gq[1 - l, k // 2], slice(P * (k % 2), P * (k % 2) + P), wq["e", l], True, True)

        def y(l, k):
            g_, t = divmod(k, 4)
            natural = vg_t[l, k][:].rearrange("p (q j) -> p q j", j=4)
            nc.vector.tensor_tensor(out=natural, in0=o_ps[l, k][:].rearrange("p (j q) -> p q j", j=4), in1=natural, op=ADD)
            nc.sync.dma_start(out=out_v[l, g_, t], in_=vg_t[l, k][:])

        def cgv(l, k):
            vg_t[l, k] = ring.tile([P, CH], F32, name="vg", tag="vg", bufs=16, align_bytes=64)
            for j in range(4):
                nc.scalar.activation(
                    out=vg_t[l, k][:, P * j : P * j + P],
                    in_=tp["g", l, k][:, P * j : P * j + P],
                    func=COPY,
                    scale=v_f[:, 4 * l + j : 4 * l + j + 1],
                )

        def ot(l, k):
            o_ps[l, k] = bank("mm")
            left, cols = gq[1 - l, k // 2], slice(P * (k % 2), P * (k % 2) + P)
            for j in range(4):
                ch = slice(P * j, P * j + P)
                nc.tensor.matmul_mx(
                    out=o_ps[l, k][:, ch],
                    lhsT=wq["e", l][0][:, ch].bitcast(FP8X4),
                    lhsT_scale=wq["e", l][1][:, ch],
                    rhs=left[0][:, cols].bitcast(FP8X4),
                    rhs_scale=left[1][:, cols],
                    start=True,
                    stop=True,
                )

        def co(l, k, eng="S"):
            oT[l, k] = ring.tile([P, CH], F32, name="o_t", tag="o_t", bufs=2, align_bytes=64)
            copy(eng, oT[l, k][:], o_ps[l, k][:])

        def ty(l, k):
            tp["y", l, k] = bank("tp")
            for j in range(4):
                ch = slice(P * j, P * j + P)
                for i, src in enumerate((vg_t[l, k], oT[l, k])):
                    nc.tensor.matmul(
                        out=tp["y", l, k][:, ch], lhsT=src[:, ch], rhs=ident[:], is_transpose=True, start=i == 0, stop=i == 1
                    )

        def yc(l, k, eng="S"):
            g_, t = divmod(k, 4)
            y_t = ring.tile([P, CH], F32, name="vg", tag="vg", bufs=16, align_bytes=64)
            copy(eng, y_t[:].rearrange("p (q j) -> p q j", j=4), tp["y", l, k][:].rearrange("p (j q) -> p q j", j=4))
            nc.sync.dma_start(out=out_v[l, g_, t], in_=y_t[:])

        def load_small():
            nc.sync.dma_start(out=a_b[:], in_=a_v)
            nc.sync.dma_start(out=v_b[:], in_=v_v)
            nc.gpsimd.tensor_copy(out=a_f[:], in_=a_b[:].rearrange("p l g t -> p (l g t)"))
            nc.gpsimd.tensor_copy(out=v_f[:], in_=v_b[:].rearrange("p l j -> p (l j)"))

        def load_v():
            nc.sync.dma_start(out=v_t[:], in_=v.rearrange("l c -> (l c)").partition_broadcast(P))

        with tc.manual_schedule():
            make_identity(nc, ident[:])
            load_x(0, 0, 2)
            load_w(("c", 0), c_v[0])
            load_x(0, 1)
            load_m(0, 0)
            load_w(("c", 1), c_v[1])
            load_x(1, 0)
            load_m(0, 1)
            load_small()
            load_x(1, 1)
            load_w(("e", 0), e_v[0])
            load_m(1, 0)
            load_m(1, 1)
            load_v()
            tx(0, 0, 0)
            tx(0, 0, 1)
            cx(0, 0, 0, "S")
            il_c(0, 1, "V")
            cx(0, 0, 1, "V")
            tx(0, 1, 1)
            il_c(0, 0, "V")
            qx(0, 0)
            tx(0, 1, 0)
            cx(0, 1, 1, "S")
            qw("c", 0)
            tm(0, 0, 0, 1)
            cx(0, 1, 0, "S")
            qx(0, 1)
            z(0, 0, 2)
            il_c(1, 0, "S")
            z(0, 1, 2)
            h(0, 0, 2)
            z(0, 1, 0)
            cm(0, 0, 0, 1)
            h(0, 1, 2)
            z(0, 0, 0)
            il_c(1, 1, "S")
            z(0, 1, 3)
            h(0, 0, 0)
            tm(0, 0, 0, 0)
            h(0, 1, 0)
            tx(1, 0, 1)
            cm(0, 0, 0, 0)
            tm(0, 1, 0, 0)
            qw("c", 1)
            cx(1, 0, 1, "S")
            z(0, 0, 3)
            qm(0, 0, 0)
            cm(0, 1, 0, 0)
            z(0, 1, 1)
            tm(0, 0, 1, 1)
            h(0, 1, 1)
            tx(1, 0, 0)
            il_e(0, 3, "G")
            cm(0, 0, 1, 1)
            h(0, 0, 3)
            tm(0, 1, 0, 1)
            cx(1, 0, 0, "S")
            il_e(0, 0, "G")
            h(0, 1, 3)
            tx(1, 1, 0)
            cm(0, 1, 0, 1)
            tm(0, 0, 1, 0)
            qx(1, 0)
            cx(1, 1, 0, "S")
            z(0, 0, 1)
            qm(0, 1, 0)
            z(1, 0, 3)
            hb(0, 1, 1, "S")
            h(0, 0, 1)
            il_e(0, 2, "G")
            z(1, 0, 2)
            cm(0, 0, 1, 0)
            h(1, 0, 3)
            il_e(0, 1, "G")
            tm(1, 0, 1, 0)
            load_w(("e", 1), e_v[1])
            hb(0, 1, 0, "S")
            h(1, 0, 2)
            hb(0, 0, 3, "G")
            hb(0, 1, 3, "S")
            z(1, 0, 0)
            qw("e", 0)
            z(1, 0, 1)
            cm(1, 0, 1, 0)
            tx(1, 1, 1)
            hb(0, 0, 0, "G")
            h(1, 0, 0)
            hb(0, 1, 2, "S")
            tm(0, 1, 1, 0)
            h(1, 0, 1)
            hb(0, 0, 2, "G")
            tm(1, 1, 0, 1)
            cx(1, 1, 1, "S")
            qh(0, 1)
            tm(1, 0, 1, 1)
            hb(1, 0, 1, "S")
            tm(0, 1, 1, 1)
            qx(1, 1)
            hb(1, 0, 2, "S")
            qm(0, 0, 1)
            z(1, 1, 2)
            hb(1, 0, 3, "S")
            z(1, 1, 3)
            il_e(1, 2, "G")
            h(1, 1, 2)
            z(1, 1, 1)
            cm(1, 0, 1, 1)
            hb(0, 0, 1, "G")
            h(1, 1, 3)
            z(1, 1, 0)
            cm(0, 1, 1, 0)
            il_e(1, 3, "G")
            h(1, 1, 1)
            tm(1, 1, 1, 0)
            hb(1, 0, 0, "S")
            h(1, 1, 0)
            il_e(1, 0, "G")
            cm(0, 1, 1, 1)
            tm(1, 0, 0, 0)
            qh(0, 0)
            cm(1, 1, 1, 0)
            tm(1, 0, 0, 1)
            qm(0, 1, 1)
            hb(1, 1, 2, "S")
            r(0, 1)
            qm(1, 0, 1)
            cm(1, 0, 0, 1)
            r(0, 7)
            g(0, 1)
            il_e(1, 1, "G")
            cm(1, 0, 0, 0)
            qh(1, 0)
            r(0, 5)
            cm(1, 1, 0, 1)
            g(0, 7)
            hb(1, 1, 0, "S")
            r(0, 2)
            qm(1, 0, 0)
            hb(1, 1, 1, "S")
            r(0, 3)
            vg(0, 7, 0, "V")
            hb(1, 1, 3, "S")
            tm(1, 1, 0, 0)
            qw("e", 1)
            g(0, 5)
            tg(0, 7)
            cm(1, 1, 0, 0)
            r(0, 6)
            qh(1, 1)
            cg(0, 7)
            r(0, 4)
            qm(1, 1, 0)
            tg(0, 5)
            g(0, 2)
            tg(0, 1)
            cgv(0, 5)
            tm(1, 1, 1, 1)
            g(0, 6)
            r(1, 0)
            cg(0, 1)
            g(0, 3)
            cm(1, 1, 1, 1)
            tg(0, 6)
            vg(0, 6, 0, "V")
            r(1, 3)
            g(1, 0)
            cg(0, 5)
            qm(1, 1, 1)
            tg(0, 2)
            cg(0, 6)
            tg(1, 0)
            cgv(0, 1)
            vg(1, 0, 0, "V")
            r(0, 0)
            g(1, 3)
            cgv(0, 2)
            tg(0, 3)
            qg(0, 6)
            tg(1, 3)
            cg(0, 2)
            g(0, 0)
            r(1, 6)
            cgv(0, 3)
            vg(1, 3, 1, "V")
            tg(0, 0)
            vg(1, 0, 1, "V")
            cg(1, 3)
            g(0, 4)
            r(1, 2)
            cg(0, 0)
            g(1, 6)
            r(1, 4)
            cgv(0, 0)
            g(1, 2)
            r(1, 1)
            cg(0, 3)
            qg(0, 0)
            tg(1, 6)
            g(1, 1)
            o(1, 0)
            cg(1, 0)
            o(1, 1)
            vg(1, 2, 1, "V")
            tg(1, 1)
            qg(0, 2)
            tg(1, 2)
            g(1, 4)
            cg(1, 1)
            r(1, 5)
            vg(1, 1, 0, "V")
            cg(1, 2)
            tg(1, 4)
            qg(1, 0)
            cg(1, 6)
            vg(1, 4, 1, "V")
            tg(0, 4)
            ot(0, 0)
            y(1, 0)
            cg(1, 4)
            vg(1, 4, 0, "V")
            ot(0, 1)
            co(0, 0)
            g(1, 5)
            co(0, 1)
            ty(0, 0)
            qg(1, 2)
            vg(1, 5, 0, "V")
            cg(0, 4)
            tg(1, 5)
            vg(1, 5, 1, "V")
            yc(0, 0)
            ot(0, 3)
            vg(1, 6, 0, "V")
            r(1, 7)
            qg(0, 4)
            cg(1, 5)
            vg(1, 6, 1, "V")
            o(1, 6)
            g(1, 7)
            co(0, 3)
            ty(0, 1)
            qg(1, 4)
            cgv(0, 4)
            ty(0, 3)
            y(1, 6)
            yc(0, 1)
            ot(0, 5)
            vg(1, 1, 1, "V")
            yc(0, 3)
            o(1, 5)
            vg(1, 7, 1, "V")
            tg(1, 7)
            y(1, 1)
            co(0, 5)
            o(1, 4)
            y(1, 5)
            ot(0, 4)
            cg(1, 7)
            ty(0, 5)
            vg(1, 3, 0, "V")
            co(0, 4)
            vg(1, 2, 0, "V")
            o(1, 2)
            y(1, 4)
            yc(0, 5)
            ot(0, 2)
            o(1, 3)
            y(1, 2)
            co(0, 2)
            ty(0, 4)
            y(1, 3)
            ty(0, 2)
            vg(0, 7, 1, "V")
            yc(0, 4)
            qg(1, 6)
            o(1, 7)
            yc(0, 2)
            vg(0, 6, 1, "V")
            o(0, 7)
            vg(1, 7, 0, "V")
            o(0, 6)
            y(0, 7)
            y(1, 7)
            y(0, 6)
